import numpy as np
import ml_dtypes


def mxq(x, axis, fmt="e4m3"):
    dtype, down = {"e4m3": (ml_dtypes.float8_e4m3fn, 7), "e5m2": (ml_dtypes.float8_e5m2, 14)}[fmt]
    v = np.moveaxis(np.asarray(x, np.float32).astype(ml_dtypes.bfloat16).astype(np.float64), axis, -1)
    blocks = v.reshape(v.shape[:-1] + (-1, 32))
    amax = np.abs(blocks).max(-1, keepdims=True)
    byte = np.maximum(np.where(amax > 0, np.frexp(amax)[1] - 1 + 127, 0) - down, 1)
    scale = np.exp2(byte - 127.0)
    codes = (blocks / scale).astype(np.float32).astype(dtype).astype(np.float64)
    return np.moveaxis((codes * scale).reshape(v.shape), -1, axis)


WIDE = False


def mx_kscale(k):
    if not WIDE:
        return np.ones(k)
    levels = np.array([10, -10, 5, -5, 0])
    if k % 512:
        return np.exp2(np.random.permutation(np.resize(levels, k // 32))).repeat(32)
    a = np.empty((k // 512, 16))
    for p in range(k // 512):
        a[p, :8] = np.random.permutation(np.resize(levels, 8))
        for g in range(8):
            far = levels[np.abs(levels - a[p, g]) >= 10]
            a[p, g + 8] = far[np.random.randint(len(far))]
    return np.exp2(a.ravel()).repeat(32)


def f64(x):
    return np.asarray(x).astype(np.float64)


def striped(idx):
    return np.tile(np.asarray(idx).reshape(-1, 16).T, (8, 1)).astype(np.uint16)


def unstriped(offs):
    return offs[:16].T.reshape(-1).astype(np.int64)


E2M1 = np.array([0.0, 0.5, 1.0, 1.5, 2.0, 3.0, 4.0, 6.0, -0.0, -0.5, -1.0, -1.5, -2.0, -3.0, -4.0, -6.0])


def pack_weight(w, fmt):
    k, n = w.shape
    w = f64(np.asarray(w, np.float32).astype(ml_dtypes.bfloat16)).reshape(k // 32, 32, n)
    amax = np.abs(w).max(1)
    if fmt == "e4m3":
        byte = np.frexp(amax)[1] - 1 + 127 - 7
    else:
        mant, ex = np.frexp(amax / 6.0)
        byte = np.where(mant > 0.5, ex, ex - 1) + 127
    byte = np.clip(np.where(amax > 0, byte, 1), 1, 254)
    scaled = (w * np.exp2(127.0 - byte)[:, None, :]).reshape(k, n).astype(np.float32)
    by_word = np.ascontiguousarray(scaled.reshape(k // 512, 128, 4, n).transpose(0, 1, 3, 2))
    if fmt == "e4m3":
        words = by_word.astype(ml_dtypes.float8_e4m3fn).view(np.uint8)
    else:
        c = by_word.astype(ml_dtypes.float4_e2m1fn).view(np.uint8) & 0xF
        words = (c[..., 0::2] | (c[..., 1::2] << 4)).reshape(k // 512, 128, 2 * n)
    return np.ascontiguousarray(words), np.ascontiguousarray(byte.astype(np.uint8).reshape(k // 512, 16, n))


def unpack_weight(words, scales, fmt):
    g, _, n = scales.shape
    words = np.ascontiguousarray(words).reshape(g, 128, n, -1)
    if fmt == "e4m3":
        vals = words.view(ml_dtypes.float8_e4m3fn).astype(np.float64)
    else:
        nib = np.empty((g, 128, n, 4), np.uint8)
        nib[..., 0::2] = words & 0xF
        nib[..., 1::2] = words >> 4
        vals = E2M1[nib]
    vals = vals * np.repeat(np.exp2(scales.astype(np.float64) - 127.0), 8, axis=1)[..., None]
    return vals.transpose(0, 1, 3, 2).reshape(g * 512, n)


def bf(x):
    return np.asarray(x, np.float32).astype(ml_dtypes.bfloat16)


def planes(Y):
    r, m = Y.shape
    b = f64(bf(Y)).reshape(r // 32, 32, m)
    amax = np.abs(b).max(1)
    byte = np.clip(np.where(amax > 0, np.frexp(amax)[1] - 1 + 127 - 7, 1), 1, 254)
    codes = (b * np.exp2(127.0 - byte)[:, None, :]).reshape(r, m).astype(np.float32).astype(ml_dtypes.float8_e4m3fn).view(np.uint8)
    words = codes.reshape(r // 512, 128, 4, m).transpose(0, 1, 3, 2)
    return np.ascontiguousarray(words), np.ascontiguousarray(byte.astype(np.uint8).reshape(r // 512, 16, m))


K, T, J, N = 512, 2048, 512, 512


def setup_inputs():
    n = np.random.standard_normal
    idx = np.random.permutation(T)[:J]
    idx2 = np.random.permutation(T)[:J]
    fj = mx_kscale(J)
    tgp = pack_weight(n((J, N)) * fj[:, None], "e2m1")
    return {
        "xf": (n((K, T))).astype(np.float32),
        "rw": (np.random.uniform(0.5, 2.0, (1, J)) / fj).astype(np.float32),
        "tg_words": tgp[0],
        "tg_scales": tgp[1],
        "old": (1.0 * n((K, N))).astype(np.float32),
        "offs": striped(idx),
        "offs2": striped(idx2),
    }


def reference(xf, rw, tg_words, tg_scales, old, offs, offs2):
    idx = unstriped(offs)
    idx2 = unstriped(offs2)
    tgu = unpack_weight(tg_words, tg_scales, "e2m1")
    d = (f64(xf)[:, idx] - f64(xf)[:, idx2]) * f64(rw)
    dt1 = d.T
    dt1q = mxq(dt1, 0, "e4m3")
    w = dt1q.T @ tgu
    y = 0.03 * w + 0.5 * f64(old)
    words, scales = planes(y)
    return y, words, scales

@@ -1,0 +1,117 @@
+from contextlib import ExitStack
+
+import concourse.mybir as mybir
+from concourse.masks import make_identity
+
+K, T, J, N = 512, 2048, 512, 512
+P = 128
+PACK = 4
+FLOPS = 2 * K * J * N
+
+F32 = mybir.dt.float32
+BF16 = mybir.dt.bfloat16
+I32 = mybir.dt.int32
+U32 = mybir.dt.uint32
+U16 = mybir.dt.uint16
+U8 = mybir.dt.uint8
+FP8X4 = mybir.dt.float8_e4m3fn_x4
+FP4X4 = mybir.dt.float4_e2m1fn_x4
+MULT = mybir.AluOpType.mult
+ADD = mybir.AluOpType.add
+COPY = mybir.ActivationFunctionType.Copy
+
+HALF = N // 2
+CHUNK = N // 4
+
+
+def tile_list_moment_of_changes_pl_kernel(tc, xf, rw, tg_words, tg_scales, old, offs, offs2, out_0, out_1, out_2):
+    nc = tc.nc
+    with ExitStack() as ctx:
+        keep = ctx.enter_context(tc.tile_pool(name="keep", bufs=1))
+        psum = ctx.enter_context(tc.psum_pool(name="psum", bufs=1))
+
+        list_a = keep.tile([P, J // 16], U16, name="list_a")
+        list_b = keep.tile([P, J // 16], U16, name="list_b")
+        nc.sync.dma_start(list_b[:], offs2)
+        nc.sync.dma_start(list_a[:], offs)
+
+        x_rows = xf.rearrange("(p t) c -> t p c", t=PACK)
+        x = [keep.tile([P, T], F32, name="x%d" % t) for t in range(PACK)]
+        for t in range(PACK):
+            nc.sync.dma_start(x[t][:], x_rows[t])
+        tg_codes = keep.tile([P, 2 * N], U8, name="tg_codes", align_bytes=64)
+        nc.sync.dma_start(tg_codes[:].bitcast(I32), tg_words[0].bitcast(I32))
+        old_rows = old.rearrange("(p t) n -> p t n", t=PACK)
+        old_pair = [keep.tile([P, 2, N], F32, name="old%d" % u) for u in range(2)]
+        for u in range(2):
+            nc.sync.dma_start(old_pair[u][:], old_rows[:, 2 * u : 2 * u + 2, :])
+
+        weight = keep.tile([P, PACK], F32, name="weight")
+        nc.scalar.dma_start(weight[:], rw.rearrange("o (q r) -> (o q) r", r=PACK))
+        tg_plane = keep.tile([P, N], U8, name="tg_plane", align_bytes=64)
+        nc.gpsimd.memset(tg_plane[:].bitcast(I32), 0)
+        for quad in range(4):
+            nc.scalar.dma_start(
+                tg_plane[32 * quad : 32 * quad + 4, :].bitcast(I32),
+                tg_scales[0, 4 * quad : 4 * quad + 4, :].bitcast(I32),
+            )
+        ident = keep.tile([P, P], F32, name="ident")
+        make_identity(nc, ident[:])
+
+        y = keep.tile([P, PACK, N], F32, name="y")
+        y_rows = out_0.rearrange("(p t) n -> t p n", t=PACK)
+        sums = []
+        for t in range(PACK):
+            minus_b = keep.tile([P, J], F32, name="minus_b%d" % t)
+            nc.vector.tensor_scalar(minus_b[:], x[t][:].indirect(list_b[:]), -1.0, 0.0, MULT, ADD)
+            plus_a = keep.tile([P, PACK, P], U32, name="plus_a%d" % t)
+            nc.vector.tensor_copy(plus_a[:].rearrange("p r q -> p q r"), x[t][:].bitcast(U32).indirect(list_a[:]))
+
+            change = psum.tile([P, PACK, P], F32, name="change%d" % t)
+            for r in range(PACK):
+                nc.tensor.matmul(change[:, r, :], minus_b[:, r::PACK], ident[:], start=(r == 0), stop=False, is_transpose=True)
+            for r in range(PACK):
+                nc.tensor.matmul(change[:, r, :], plus_a[:, r, :].bitcast(F32), ident[:], start=False, stop=(r == PACK - 1), is_transpose=True)
+
+            dt1 = keep.tile([P, P, PACK], BF16, name="dt1_%d" % t, align_bytes=64)
+            if t < PACK - 1:
+                for r in range(PACK):
+                    nc.scalar.activation(dt1[:, :, r], change[:, r, :], COPY, scale=weight[:, r : r + 1])
+            else:
+                nc.vector.tensor_tensor(
+                    dt1[:], change[:].rearrange("q r m -> q m r"), weight[:].unsqueeze(1).to_broadcast([P, P, PACK]), MULT
+                )
+            codes = keep.tile([P, P], U32, name="codes%d" % t, align_bytes=64)
+            plane = keep.tile([P, P], U8, name="plane%d" % t, align_bytes=64)
+            nc.vector.quantize_mx(out=codes[:].bitcast(FP8X4), scales=plane[:], in_=dt1[:].rearrange("q m r -> q (m r)"))
+
+            w = psum.tile([P, N], F32, name="w%d" % t)
+            nc.tensor.matmul_mx(
+                out=w[:], lhsT=codes[:].bitcast(FP8X4), lhsT_scale=plane[:],
+                rhs=tg_codes[:].bitcast(FP4X4), rhs_scale=tg_plane[:], start=True, stop=True,
+            )
+            sums.append(w)
+
+        for t in range(PACK):
+            half_old = keep.tile([P, N], F32, name="half_old%d" % t)
+            nc.scalar.activation(half_old[:], old_pair[t // 2][:, t % 2, :], COPY, scale=0.5)
+            nc.vector.scalar_tensor_tensor(y[:, t, :], sums[t][:], 0.03, half_old[:], MULT, ADD)
+            nc.sync.dma_start(y_rows[t], y[:, t, :])
+
+        y_codes = keep.tile([P, N], U32, name="y_codes", align_bytes=64)
+        y_plane = keep.tile([P, N], U8, name="y_plane", align_bytes=64)
+        for h in range(2):
+            cols = slice(h * HALF, (h + 1) * HALF)
+            y_bf = keep.tile([P, HALF, PACK], BF16, name="y_bf%d" % h, align_bytes=64)
+            if h == 1:
+                nc.scalar.copy(y_bf[:], y[:, :, cols].rearrange("p t n -> p n t"))
+            else:
+                nc.vector.tensor_copy(y_bf[:], y[:, :, cols].rearrange("p t n -> p n t"))
+            nc.vector.quantize_mx(out=y_codes[:, cols].bitcast(FP8X4), scales=y_plane[:, cols], in_=y_bf[:].rearrange("p n t -> p (n t)"))
+        nc.sync.dma_start(out_1[0].rearrange("p n t -> p (n t)").bitcast(I32), y_codes[:].bitcast(I32))
+        for quad in range(4):
+            queue = nc.sync if quad % 2 else nc.scalar
+            queue.dma_start(
+                out_2[0, 4 * quad : 4 * quad + 4, :].bitcast(I32),
+                y_plane[32 * quad : 32 * quad + 4, :].bitcast(I32),
+            )

@@ -36,15 +36,17 @@ def tile_list_moment_of_changes_pl_kernel(tc, xf, rw, tg_words, tg_scales, old, 
         nc.sync.dma_start(list_a[:], offs)
 
         x_rows = xf.rearrange("(p t) c -> t p c", t=PACK)
-        x = [keep.tile([P, T], F32, name="x%d" % t) for t in range(PACK)]
-        for t in range(PACK):
-            nc.sync.dma_start(x[t][:], x_rows[t])
-        tg_codes = keep.tile([P, 2 * N], U8, name="tg_codes", align_bytes=64)
-        nc.sync.dma_start(tg_codes[:].bitcast(I32), tg_words[0].bitcast(I32))
         old_rows = old.rearrange("(p t) n -> p t n", t=PACK)
-        old_pair = [keep.tile([P, 2, N], F32, name="old%d" % u) for u in range(2)]
-        for u in range(2):
-            nc.sync.dma_start(old_pair[u][:], old_rows[:, 2 * u : 2 * u + 2, :])
+        x = [keep.tile([P, T], F32, name="x%d" % t, tag="x%d" % t, align_bytes=64) for t in range(PACK)]
+        old_first = keep.tile([P, N], F32, name="old_first")
+        old_rest = keep.tile([P, PACK - 1, N], F32, name="old_rest")
+        tg_codes = keep.tile([P, 2 * N], U8, name="tg_codes", align_bytes=64)
+        for t in range(PACK - 1):
+            nc.sync.dma_start(x[t][:], x_rows[t])
+        nc.sync.dma_start(old_first[:], old_rows[:, 0, :])
+        nc.sync.dma_start(x[PACK - 1][:], x_rows[PACK - 1])
+        nc.sync.dma_start(tg_codes[:].bitcast(I32), tg_words[0].bitcast(I32))
+        nc.sync.dma_start(old_rest[:], old_rows[:, 1:PACK, :])
 
         weight = keep.tile([P, PACK], F32, name="weight")
         nc.scalar.dma_start(weight[:], rw.rearrange("o (q r) -> (o q) r", r=PACK))
@@ -58,57 +60,104 @@ def tile_list_moment_of_changes_pl_kernel(tc, xf, rw, tg_words, tg_scales, old, 
         ident = keep.tile([P, P], F32, name="ident")
         make_identity(nc, ident[:])
 
-        y = keep.tile([P, PACK, N], F32, name="y")
-        y_rows = out_0.rearrange("(p t) n -> t p n", t=PACK)
-        sums = []
+        changes = []
         for t in range(PACK):
             minus_b = keep.tile([P, J], F32, name="minus_b%d" % t)
             nc.vector.tensor_scalar(minus_b[:], x[t][:].indirect(list_b[:]), -1.0, 0.0, MULT, ADD)
             plus_a = keep.tile([P, PACK, P], U32, name="plus_a%d" % t)
             nc.vector.tensor_copy(plus_a[:].rearrange("p r q -> p q r"), x[t][:].bitcast(U32).indirect(list_a[:]))
 
-            change = psum.tile([P, PACK, P], F32, name="change%d" % t)
+            change = psum.tile([P, PACK, P], F32, name="change%d" % t, tag="bank%d" % t)
             for r in range(PACK):
                 nc.tensor.matmul(change[:, r, :], minus_b[:, r::PACK], ident[:], start=(r == 0), stop=False, is_transpose=True)
             for r in range(PACK):
                 nc.tensor.matmul(change[:, r, :], plus_a[:, r, :].bitcast(F32), ident[:], start=False, stop=(r == PACK - 1), is_transpose=True)
+            changes.append(change)
 
-            dt1 = keep.tile([P, P, PACK], BF16, name="dt1_%d" % t, align_bytes=64)
-            if t < PACK - 1:
-                for r in range(PACK):
-                    nc.scalar.activation(dt1[:, :, r], change[:, r, :], COPY, scale=weight[:, r : r + 1])
-            else:
-                nc.vector.tensor_tensor(
-                    dt1[:], change[:].rearrange("q r m -> q m r"), weight[:].unsqueeze(1).to_broadcast([P, P, PACK]), MULT
-                )
-            codes = keep.tile([P, P], U32, name="codes%d" % t, align_bytes=64)
+        y = keep.tile([P, PACK, N], F32, name="y")
+        y_rows = out_0.rearrange("(p t) n -> t p n", t=PACK)
+        y_bf = [keep.tile([P, HALF, PACK], BF16, name="y_bf%d" % h, align_bytes=64) for h in range(2)]
+        halves = [slice(h * HALF, (h + 1) * HALF) for h in range(2)]
+        dt1 = [keep.tile([P, P, PACK], BF16, name="dt1_%d" % t, align_bytes=64) for t in range(PACK)]
+        half_old = [keep.tile([P, N], F32, name="half_old%d" % t, tag="half_old%d" % t, align_bytes=64) for t in range(PACK)]
+        code_tags = ["x2", "x3", "half_old0", "codes3"]
+        operands = {}
+        sums = {}
+
+        def weigh_on_scalar(t):
+            for r in range(PACK):
+                nc.scalar.activation(dt1[t][:, :, r], changes[t][:, r, :], COPY, scale=weight[:, r : r + 1])
+
+        def weigh_on_vector(t):
+            nc.vector.tensor_tensor(
+                dt1[t][:], changes[t][:].rearrange("q r m -> q m r"), weight[:].unsqueeze(1).to_broadcast([P, P, PACK]), MULT
+            )
+
+        def halve(t):
+            src = old_first[:] if t == 0 else old_rest[:, t - 1, :]
+            nc.scalar.activation(half_old[t][:], src, COPY, scale=0.5)
+
+        def quantise(t):
+            codes = keep.tile([P, P], U32, name="codes%d" % t, tag=code_tags[t], align_bytes=64)
             plane = keep.tile([P, P], U8, name="plane%d" % t, align_bytes=64)
-            nc.vector.quantize_mx(out=codes[:].bitcast(FP8X4), scales=plane[:], in_=dt1[:].rearrange("q m r -> q (m r)"))
+            nc.vector.quantize_mx(out=codes[:].bitcast(FP8X4), scales=plane[:], in_=dt1[t][:].rearrange("q m r -> q (m r)"))
+            operands[t] = (codes, plane)
 
-            w = psum.tile([P, N], F32, name="w%d" % t)
+        def multiply(t, n0, n1, bank):
+            codes, plane = operands[t]
+            w = psum.tile([P, n1 - n0], F32, name="w%d_%d" % (t, n0), tag=bank)
             nc.tensor.matmul_mx(
                 out=w[:], lhsT=codes[:].bitcast(FP8X4), lhsT_scale=plane[:],
-                rhs=tg_codes[:].bitcast(FP4X4), rhs_scale=tg_plane[:], start=True, stop=True,
+                rhs=tg_codes[:, 2 * n0 : 2 * n1].bitcast(FP4X4), rhs_scale=tg_plane[:, n0:n1], start=True, stop=True,
             )
-            sums.append(w)
+            sums[(t, n0)] = w
 
-        for t in range(PACK):
-            half_old = keep.tile([P, N], F32, name="half_old%d" % t)
-            nc.scalar.activation(half_old[:], old_pair[t // 2][:, t % 2, :], COPY, scale=0.5)
-            nc.vector.scalar_tensor_tensor(y[:, t, :], sums[t][:], 0.03, half_old[:], MULT, ADD)
+        def combine(t, n0, n1):
+            nc.vector.scalar_tensor_tensor(y[:, t, n0:n1], sums[(t, n0)][:], 0.03, half_old[t][:, n0:n1], MULT, ADD)
+
+        def store(t):
             nc.sync.dma_start(y_rows[t], y[:, t, :])
+
+        def round_pair(copy, u, h):
+            copy(y_bf[h][:, :, 2 * u : 2 * u + 2], y[:, 2 * u : 2 * u + 2, halves[h]].rearrange("p t n -> p n t"))
+
+        weigh_on_scalar(0)
+        weigh_on_scalar(1)
+        halve(0)
+        weigh_on_scalar(2)
+        quantise(0)
+        multiply(0, 0, N, "bank4")
+        quantise(1)
+        multiply(1, 0, N, "bank5")
+        combine(0, 0, N)
+        store(0)
+        weigh_on_vector(3)
+        quantise(2)
+        quantise(3)
+        multiply(2, 0, N, "bank6")
+        multiply(3, 0, HALF, "bank7")
+        multiply(3, HALF, N, "bank0")
+        for t in range(1, PACK):
+            halve(t)
+        combine(1, 0, N)
+        store(1)
+        round_pair(nc.scalar.copy, 0, 1)
+        round_pair(nc.scalar.copy, 0, 0)
+        combine(2, 0, N)
+        store(2)
+        combine(3, 0, HALF)
+        combine(3, HALF, N)
+        store(3)
+        round_pair(nc.scalar.copy, 1, 0)
+        round_pair(nc.vector.tensor_copy, 1, 1)
 
         y_codes = keep.tile([P, N], U32, name="y_codes", align_bytes=64)
         y_plane = keep.tile([P, N], U8, name="y_plane", align_bytes=64)
-        for h in range(2):
-            cols = slice(h * HALF, (h + 1) * HALF)
-            y_bf = keep.tile([P, HALF, PACK], BF16, name="y_bf%d" % h, align_bytes=64)
-            if h == 1:
-                nc.scalar.copy(y_bf[:], y[:, :, cols].rearrange("p t n -> p n t"))
-            else:
-                nc.vector.tensor_copy(y_bf[:], y[:, :, cols].rearrange("p t n -> p n t"))
-            nc.vector.quantize_mx(out=y_codes[:, cols].bitcast(FP8X4), scales=y_plane[:, cols], in_=y_bf[:].rearrange("p n t -> p (n t)"))
-        nc.sync.dma_start(out_1[0].rearrange("p n t -> p (n t)").bitcast(I32), y_codes[:].bitcast(I32))
+        words_out = out_1[0].rearrange("p n t -> p (n t)").bitcast(I32)
+        for h in (1, 0):
+            cols = halves[h]
+            nc.vector.quantize_mx(out=y_codes[:, cols].bitcast(FP8X4), scales=y_plane[:, cols], in_=y_bf[h][:].rearrange("p n t -> p (n t)"))
+            nc.sync.dma_start(words_out[:, cols], y_codes[:, cols].bitcast(I32))
         for quad in range(4):
             queue = nc.sync if quad % 2 else nc.scalar
             queue.dma_start(

@@ -32,31 +32,30 @@ def tile_list_moment_of_changes_pl_kernel(tc, xf, rw, tg_words, tg_scales, old, 
 
         list_a = keep.tile([P, J // 16], U16, name="list_a")
         list_b = keep.tile([P, J // 16], U16, name="list_b")
-        nc.sync.dma_start(list_b[:], offs2)
-        nc.sync.dma_start(list_a[:], offs)
 
         x_rows = xf.rearrange("(p t) c -> t p c", t=PACK)
         old_rows = old.rearrange("(p t) n -> p t n", t=PACK)
         x = [keep.tile([P, T], F32, name="x%d" % t, tag="x%d" % t, align_bytes=64) for t in range(PACK)]
-        old_first = keep.tile([P, N], F32, name="old_first")
-        old_rest = keep.tile([P, PACK - 1, N], F32, name="old_rest")
+        old_pair = [keep.tile([P, 2, N], F32, name="old%d" % u) for u in range(2)]
         tg_codes = keep.tile([P, 2 * N], U8, name="tg_codes", align_bytes=64)
-        for t in range(PACK - 1):
-            nc.sync.dma_start(x[t][:], x_rows[t])
-        nc.sync.dma_start(old_first[:], old_rows[:, 0, :])
-        nc.sync.dma_start(x[PACK - 1][:], x_rows[PACK - 1])
-        nc.sync.dma_start(tg_codes[:].bitcast(I32), tg_words[0].bitcast(I32))
-        nc.sync.dma_start(old_rest[:], old_rows[:, 1:PACK, :])
-
         weight = keep.tile([P, PACK], F32, name="weight")
-        nc.scalar.dma_start(weight[:], rw.rearrange("o (q r) -> (o q) r", r=PACK))
         tg_plane = keep.tile([P, N], U8, name="tg_plane", align_bytes=64)
         nc.gpsimd.memset(tg_plane[:].bitcast(I32), 0)
+        nc.sync.dma_start(x[0][:], x_rows[0])
+        nc.sync.dma_start(list_b[:], offs2)
+        nc.sync.dma_start(list_a[:], offs)
+        nc.sync.dma_start(x[1][:], x_rows[1])
+        nc.sync.dma_start(weight[:], rw.rearrange("o (q r) -> (o q) r", r=PACK))
+        for t in range(2, PACK):
+            nc.sync.dma_start(x[t][:], x_rows[t])
+        nc.sync.dma_start(tg_codes[:].bitcast(I32), tg_words[0].bitcast(I32))
         for quad in range(4):
-            nc.scalar.dma_start(
+            nc.sync.dma_start(
                 tg_plane[32 * quad : 32 * quad + 4, :].bitcast(I32),
                 tg_scales[0, 4 * quad : 4 * quad + 4, :].bitcast(I32),
             )
+        for u in range(2):
+            nc.sync.dma_start(old_pair[u][:], old_rows[:, 2 * u : 2 * u + 2, :])
         ident = keep.tile([P, P], F32, name="ident")
         make_identity(nc, ident[:])
 
@@ -64,50 +63,49 @@ def tile_list_moment_of_changes_pl_kernel(tc, xf, rw, tg_words, tg_scales, old, 
         for t in range(PACK):
             minus_b = keep.tile([P, J], F32, name="minus_b%d" % t)
             nc.vector.tensor_scalar(minus_b[:], x[t][:].indirect(list_b[:]), -1.0, 0.0, MULT, ADD)
-            plus_a = keep.tile([P, PACK, P], U32, name="plus_a%d" % t)
-            nc.vector.tensor_copy(plus_a[:].rearrange("p r q -> p q r"), x[t][:].bitcast(U32).indirect(list_a[:]))
+            plus_a = keep.tile([P, J], F32, name="plus_a%d" % t)
+            nc.vector.tensor_copy(plus_a[:], x[t][:].indirect(list_a[:]))
 
             change = psum.tile([P, PACK, P], F32, name="change%d" % t, tag="bank%d" % t)
             for r in range(PACK):
                 nc.tensor.matmul(change[:, r, :], minus_b[:, r::PACK], ident[:], start=(r == 0), stop=False, is_transpose=True)
             for r in range(PACK):
-                nc.tensor.matmul(change[:, r, :], plus_a[:, r, :].bitcast(F32), ident[:], start=False, stop=(r == PACK - 1), is_transpose=True)
+                nc.tensor.matmul(change[:, r, :], plus_a[:, r::PACK], ident[:], start=False, stop=(r == PACK - 1), is_transpose=True)
             changes.append(change)
 
         y = keep.tile([P, PACK, N], F32, name="y")
         y_rows = out_0.rearrange("(p t) n -> t p n", t=PACK)
         y_bf = [keep.tile([P, HALF, PACK], BF16, name="y_bf%d" % h, align_bytes=64) for h in range(2)]
         halves = [slice(h * HALF, (h + 1) * HALF) for h in range(2)]
-        dt1 = [keep.tile([P, P, PACK], BF16, name="dt1_%d" % t, align_bytes=64) for t in range(PACK)]
+        dt1 = keep.tile([P, PACK, P, PACK], BF16, name="dt1", align_bytes=64)
         half_old = [keep.tile([P, N], F32, name="half_old%d" % t, tag="half_old%d" % t, align_bytes=64) for t in range(PACK)]
-        code_tags = ["x2", "x3", "half_old0", "codes3"]
-        operands = {}
+        early_codes = keep.tile([P, (PACK - 1) * P], U32, name="early_codes", tag="x3", align_bytes=64)
+        last_codes = keep.tile([P, P], U32, name="last_codes", tag="half_old0", align_bytes=64)
+        planes = keep.tile([P, PACK * P], U8, name="planes", align_bytes=64)
+        codes = [early_codes[:, t * P : (t + 1) * P] for t in range(PACK - 1)] + [last_codes[:]]
         sums = {}
 
         def weigh_on_scalar(t):
             for r in range(PACK):
-                nc.scalar.activation(dt1[t][:, :, r], changes[t][:, r, :], COPY, scale=weight[:, r : r + 1])
+                nc.scalar.activation(dt1[:, t, :, r], changes[t][:, r, :], COPY, scale=weight[:, r : r + 1])
 
         def weigh_on_vector(t):
             nc.vector.tensor_tensor(
-                dt1[t][:], changes[t][:].rearrange("q r m -> q m r"), weight[:].unsqueeze(1).to_broadcast([P, P, PACK]), MULT
+                dt1[:, t], changes[t][:].rearrange("q r m -> q m r"), weight[:].unsqueeze(1).to_broadcast([P, P, PACK]), MULT
             )
 
         def halve(t):
-            src = old_first[:] if t == 0 else old_rest[:, t - 1, :]
-            nc.scalar.activation(half_old[t][:], src, COPY, scale=0.5)
+            nc.scalar.activation(half_old[t][:], old_pair[t // 2][:, t % 2, :], COPY, scale=0.5)
 
-        def quantise(t):
-            codes = keep.tile([P, P], U32, name="codes%d" % t, tag=code_tags[t], align_bytes=64)
-            plane = keep.tile([P, P], U8, name="plane%d" % t, align_bytes=64)
-            nc.vector.quantize_mx(out=codes[:].bitcast(FP8X4), scales=plane[:], in_=dt1[t][:].rearrange("q m r -> q (m r)"))
-            operands[t] = (codes, plane)
+        def quantise(out, t0, t1):
+            nc.vector.quantize_mx(
+                out=out.bitcast(FP8X4), scales=planes[:, t0 * P : t1 * P], in_=dt1[:, t0:t1].rearrange("q t m r -> q (t m r)")
+            )
 
         def multiply(t, n0, n1, bank):
-            codes, plane = operands[t]
             w = psum.tile([P, n1 - n0], F32, name="w%d_%d" % (t, n0), tag=bank)
             nc.tensor.matmul_mx(
-                out=w[:], lhsT=codes[:].bitcast(FP8X4), lhsT_scale=plane[:],
+                out=w[:], lhsT=codes[t].bitcast(FP8X4), lhsT_scale=planes[:, t * P : (t + 1) * P],
                 rhs=tg_codes[:, 2 * n0 : 2 * n1].bitcast(FP4X4), rhs_scale=tg_plane[:, n0:n1], start=True, stop=True,
             )
             sums[(t, n0)] = w
@@ -118,43 +116,42 @@ def tile_list_moment_of_changes_pl_kernel(tc, xf, rw, tg_words, tg_scales, old, 
         def store(t):
             nc.sync.dma_start(y_rows[t], y[:, t, :])
 
-        def round_pair(copy, u, h):
-            copy(y_bf[h][:, :, 2 * u : 2 * u + 2], y[:, 2 * u : 2 * u + 2, halves[h]].rearrange("p t n -> p n t"))
+        def round_pair(copy, u, h, c0=0, c1=HALF):
+            n0 = h * HALF
+            copy(y_bf[h][:, c0:c1, 2 * u : 2 * u + 2], y[:, 2 * u : 2 * u + 2, n0 + c0 : n0 + c1].rearrange("p t n -> p n t"))
 
-        weigh_on_scalar(0)
-        weigh_on_scalar(1)
-        halve(0)
-        weigh_on_scalar(2)
-        quantise(0)
+        for t in range(PACK - 1):
+            weigh_on_scalar(t)
+        for t in range(PACK):
+            halve(t)
+        quantise(early_codes[:, 0 : 2 * P], 0, 2)
+        quantise(early_codes[:, 2 * P : 3 * P], 2, 3)
+        weigh_on_vector(3)
         multiply(0, 0, N, "bank4")
-        quantise(1)
         multiply(1, 0, N, "bank5")
+        multiply(2, 0, N, "bank6")
         combine(0, 0, N)
         store(0)
-        weigh_on_vector(3)
-        quantise(2)
-        quantise(3)
-        multiply(2, 0, N, "bank6")
-        multiply(3, 0, HALF, "bank7")
-        multiply(3, HALF, N, "bank0")
-        for t in range(1, PACK):
-            halve(t)
         combine(1, 0, N)
         store(1)
-        round_pair(nc.scalar.copy, 0, 1)
+        quantise(last_codes[:], 3, 4)
+        multiply(3, 0, HALF, "bank7")
+        multiply(3, HALF, N, "bank0")
         round_pair(nc.scalar.copy, 0, 0)
+        round_pair(nc.scalar.copy, 0, 1)
         combine(2, 0, N)
         store(2)
         combine(3, 0, HALF)
         combine(3, HALF, N)
         store(3)
-        round_pair(nc.scalar.copy, 1, 0)
-        round_pair(nc.vector.tensor_copy, 1, 1)
+        round_pair(nc.vector.tensor_copy, 1, 0)
+        round_pair(nc.vector.tensor_copy, 1, 1, 0, CHUNK)
+        round_pair(nc.scalar.copy, 1, 1, CHUNK, HALF)
 
         y_codes = keep.tile([P, N], U32, name="y_codes", align_bytes=64)
         y_plane = keep.tile([P, N], U8, name="y_plane", align_bytes=64)
         words_out = out_1[0].rearrange("p n t -> p (n t)").bitcast(I32)
-        for h in (1, 0):
+        for h in range(2):
             cols = halves[h]
             nc.vector.quantize_mx(out=y_codes[:, cols].bitcast(FP8X4), scales=y_plane[:, cols], in_=y_bf[h][:].rearrange("p n t -> p (n t)"))
             nc.sync.dma_start(words_out[:, cols], y_codes[:, cols].bitcast(I32))

from contextlib import ExitStack

import concourse.mybir as mybir
from concourse.masks import make_identity

K, T, J, N = 512, 2048, 512, 512
P = 128
PACK = 4
FLOPS = 2 * K * J * N

F32 = mybir.dt.float32
BF16 = mybir.dt.bfloat16
I32 = mybir.dt.int32
U32 = mybir.dt.uint32
U16 = mybir.dt.uint16
U8 = mybir.dt.uint8
FP8X4 = mybir.dt.float8_e4m3fn_x4
FP4X4 = mybir.dt.float4_e2m1fn_x4
MULT = mybir.AluOpType.mult
ADD = mybir.AluOpType.add
COPY = mybir.ActivationFunctionType.Copy

HALF = N // 2
CHUNK = N // 4


def tile_list_moment_of_changes_pl_kernel(tc, xf, rw, tg_words, tg_scales, old, offs, offs2, out_0, out_1, out_2):
    nc = tc.nc
    with ExitStack() as ctx:
        keep = ctx.enter_context(tc.tile_pool(name="keep", bufs=1))
        psum = ctx.enter_context(tc.psum_pool(name="psum", bufs=1))

        list_a = keep.tile([P, J // 16], U16, name="list_a")
        list_b = keep.tile([P, J // 16], U16, name="list_b")

        x_rows = xf.rearrange("(p t) c -> t p c", t=PACK)
        old_rows = old.rearrange("(p t) n -> p t n", t=PACK)
        x = [keep.tile([P, T], F32, name="x%d" % t, tag="x%d" % t, align_bytes=64) for t in range(PACK)]
        old_pair = [keep.tile([P, 2, N], F32, name="old%d" % u) for u in range(2)]
        tg_codes = keep.tile([P, 2 * N], U8, name="tg_codes", align_bytes=64)
        weight = keep.tile([P, PACK], F32, name="weight")
        tg_plane = keep.tile([P, N], U8, name="tg_plane", align_bytes=64)
        nc.gpsimd.memset(tg_plane[:].bitcast(I32), 0)
        nc.sync.dma_start(x[0][:], x_rows[0])
        nc.sync.dma_start(list_b[:], offs2)
        nc.sync.dma_start(list_a[:], offs)
        nc.sync.dma_start(x[1][:], x_rows[1])
        nc.sync.dma_start(weight[:], rw.rearrange("o (q r) -> (o q) r", r=PACK))
        for t in range(2, PACK):
            nc.sync.dma_start(x[t][:], x_rows[t])
        nc.sync.dma_start(tg_codes[:].bitcast(I32), tg_words[0].bitcast(I32))
        for quad in range(4):
            nc.sync.dma_start(
                tg_plane[32 * quad : 32 * quad + 4, :].bitcast(I32),
                tg_scales[0, 4 * quad : 4 * quad + 4, :].bitcast(I32),
            )
        for u in range(2):
            nc.sync.dma_start(old_pair[u][:], old_rows[:, 2 * u : 2 * u + 2, :])
        ident = keep.tile([P, P], F32, name="ident")
        make_identity(nc, ident[:])

        changes = []
        for t in range(PACK):
            minus_b = keep.tile([P, J], F32, name="minus_b%d" % t)
            nc.vector.tensor_scalar(minus_b[:], x[t][:].indirect(list_b[:]), -1.0, 0.0, MULT, ADD)
            plus_a = keep.tile([P, J], F32, name="plus_a%d" % t)
            nc.vector.tensor_copy(plus_a[:], x[t][:].indirect(list_a[:]))

            change = psum.tile([P, PACK, P], F32, name="change%d" % t, tag="bank%d" % t)
            for r in range(PACK):
                nc.tensor.matmul(change[:, r, :], minus_b[:, r::PACK], ident[:], start=(r == 0), stop=False, is_transpose=True)
            for r in range(PACK):
                nc.tensor.matmul(change[:, r, :], plus_a[:, r::PACK], ident[:], start=False, stop=(r == PACK - 1), is_transpose=True)
            changes.append(change)

        y = keep.tile([P, PACK, N], F32, name="y")
        y_rows = out_0.rearrange("(p t) n -> t p n", t=PACK)
        y_bf = [keep.tile([P, HALF, PACK], BF16, name="y_bf%d" % h, align_bytes=64) for h in range(2)]
        halves = [slice(h * HALF, (h + 1) * HALF) for h in range(2)]
        dt1 = keep.tile([P, PACK, P, PACK], BF16, name="dt1", align_bytes=64)
        half_old = [keep.tile([P, N], F32, name="half_old%d" % t, tag="half_old%d" % t, align_bytes=64) for t in range(PACK)]
        early_codes = keep.tile([P, (PACK - 1) * P], U32, name="early_codes", tag="x3", align_bytes=64)
        last_codes = keep.tile([P, P], U32, name="last_codes", tag="half_old0", align_bytes=64)
        planes = keep.tile([P, PACK * P], U8, name="planes", align_bytes=64)
        codes = [early_codes[:, t * P : (t + 1) * P] for t in range(PACK - 1)] + [last_codes[:]]
        sums = {}

        def weigh_on_scalar(t):
            for r in range(PACK):
                nc.scalar.activation(dt1[:, t, :, r], changes[t][:, r, :], COPY, scale=weight[:, r : r + 1])

        def weigh_on_vector(t):
            nc.vector.tensor_tensor(
                dt1[:, t], changes[t][:].rearrange("q r m -> q m r"), weight[:].unsqueeze(1).to_broadcast([P, P, PACK]), MULT
            )

        def halve(t):
            nc.scalar.activation(half_old[t][:], old_pair[t // 2][:, t % 2, :], COPY, scale=0.5)

        def quantise(out, t0, t1):
            nc.vector.quantize_mx(
                out=out.bitcast(FP8X4), scales=planes[:, t0 * P : t1 * P], in_=dt1[:, t0:t1].rearrange("q t m r -> q (t m r)")
            )

        def multiply(t, n0, n1, bank):
            w = psum.tile([P, n1 - n0], F32, name="w%d_%d" % (t, n0), tag=bank)
            nc.tensor.matmul_mx(
                out=w[:], lhsT=codes[t].bitcast(FP8X4), lhsT_scale=planes[:, t * P : (t + 1) * P],
                rhs=tg_codes[:, 2 * n0 : 2 * n1].bitcast(FP4X4), rhs_scale=tg_plane[:, n0:n1], start=True, stop=True,
            )
            sums[(t, n0)] = w

        def combine(t, n0, n1):
            nc.vector.scalar_tensor_tensor(y[:, t, n0:n1], sums[(t, n0)][:], 0.03, half_old[t][:, n0:n1], MULT, ADD)

        def store(t):
            nc.sync.dma_start(y_rows[t], y[:, t, :])

        def round_pair(copy, u, h, c0=0, c1=HALF):
            n0 = h * HALF
            copy(y_bf[h][:, c0:c1, 2 * u : 2 * u + 2], y[:, 2 * u : 2 * u + 2, n0 + c0 : n0 + c1].rearrange("p t n -> p n t"))

        for t in range(PACK - 1):
            weigh_on_scalar(t)
        for t in range(PACK):
            halve(t)
        quantise(early_codes[:, 0 : 2 * P], 0, 2)
        quantise(early_codes[:, 2 * P : 3 * P], 2, 3)
        weigh_on_vector(3)
        multiply(0, 0, N, "bank4")
        multiply(1, 0, N, "bank5")
        multiply(2, 0, N, "bank6")
        combine(0, 0, N)
        store(0)
        combine(1, 0, N)
        store(1)
        quantise(last_codes[:], 3, 4)
        multiply(3, 0, HALF, "bank7")
        multiply(3, HALF, N, "bank0")
        round_pair(nc.scalar.copy, 0, 0)
        round_pair(nc.scalar.copy, 0, 1)
        combine(2, 0, N)
        store(2)
        combine(3, 0, HALF)
        combine(3, HALF, N)
        store(3)
        round_pair(nc.vector.tensor_copy, 1, 0)
        round_pair(nc.vector.tensor_copy, 1, 1, 0, CHUNK)
        round_pair(nc.scalar.copy, 1, 1, CHUNK, HALF)

        y_codes = keep.tile([P, N], U32, name="y_codes", align_bytes=64)
        y_plane = keep.tile([P, N], U8, name="y_plane", align_bytes=64)
        words_out = out_1[0].rearrange("p n t -> p (n t)").bitcast(I32)
        for h in range(2):
            cols = halves[h]
            nc.vector.quantize_mx(out=y_codes[:, cols].bitcast(FP8X4), scales=y_plane[:, cols], in_=y_bf[h][:].rearrange("p n t -> p (n t)"))
            nc.sync.dma_start(words_out[:, cols], y_codes[:, cols].bitcast(I32))
        for quad in range(4):
            queue = nc.sync if quad % 2 else nc.scalar
            queue.dma_start(
                out_2[0, 4 * quad : 4 * quad + 4, :].bitcast(I32),
                y_plane[32 * quad : 32 * quad + 4, :].bitcast(I32),
            )
